import numpy as np
import ml_dtypes


def mxq(x, axis, fmt="e4m3"):
    dtype, down = {"e4m3": (ml_dtypes.float8_e4m3fn, 7), "e5m2": (ml_dtypes.float8_e5m2, 14)}[fmt]
    v = np.moveaxis(np.asarray(x, np.float32).astype(ml_dtypes.bfloat16).astype(np.float64), axis, -1)
    blocks = v.reshape(v.shape[:-1] + (-1, 32))
    amax = np.abs(blocks).max(-1, keepdims=True)
    byte = np.maximum(np.where(amax > 0, np.frexp(amax)[1] - 1 + 127, 0) - down, 1)
    scale = np.exp2(byte - 127.0)
    codes = (blocks / scale).astype(np.float32).astype(dtype).astype(np.float64)
    return np.moveaxis((codes * scale).reshape(v.shape), -1, axis)


WIDE = False


def mx_kscale(k):
    if not WIDE:
        return np.ones(k)
    levels = np.array([10, -10, 5, -5, 0])
    if k % 512:
        return np.exp2(np.random.permutation(np.resize(levels, k // 32))).repeat(32)
    a = np.empty((k // 512, 16))
    for p in range(k // 512):
        a[p, :8] = np.random.permutation(np.resize(levels, 8))
        for g in range(8):
            far = levels[np.abs(levels - a[p, g]) >= 10]
            a[p, g + 8] = far[np.random.randint(len(far))]
    return np.exp2(a.ravel()).repeat(32)


BF16 = ml_dtypes.bfloat16


def bf(x):
    return np.asarray(x, np.float32).astype(BF16)


def f64(x):
    return np.asarray(x).astype(np.float64)


E2M1 = np.array([0.0, 0.5, 1.0, 1.5, 2.0, 3.0, 4.0, 6.0, -0.0, -0.5, -1.0, -1.5, -2.0, -3.0, -4.0, -6.0])


def pack_weight(w, fmt):
    k, n = w.shape
    w = f64(bf(w)).reshape(k // 32, 32, n)
    amax = np.abs(w).max(1)
    if fmt == "e4m3":
        byte = np.frexp(amax)[1] - 1 + 127 - 7
    else:
        mant, ex = np.frexp(amax / 6.0)
        byte = np.where(mant > 0.5, ex, ex - 1) + 127
    byte = np.clip(np.where(amax > 0, byte, 1), 1, 254)
    scaled = (w * np.exp2(127.0 - byte)[:, None, :]).reshape(k, n).astype(np.float32)
    by_word = np.ascontiguousarray(scaled.reshape(k // 512, 128, 4, n).transpose(0, 1, 3, 2))
    if fmt == "e4m3":
        words = by_word.astype(ml_dtypes.float8_e4m3fn).view(np.uint8)
    else:
        c = by_word.astype(ml_dtypes.float4_e2m1fn).view(np.uint8) & 0xF
        words = c[..., 0::2] | (c[..., 1::2] << 4)
    return np.ascontiguousarray(words), np.ascontiguousarray(byte.astype(np.uint8).reshape(k // 512, 16, n))


def unpack_weight(words, scales, fmt):
    g, p, n, _ = words.shape
    if fmt == "e4m3":
        vals = np.ascontiguousarray(words).view(ml_dtypes.float8_e4m3fn).astype(np.float64)
    else:
        nib = np.empty((g, p, n, 4), np.uint8)
        nib[..., 0::2] = words & 0xF
        nib[..., 1::2] = words >> 4
        vals = E2M1[nib]
    vals = vals * np.repeat(np.exp2(scales.astype(np.float64) - 127.0), 8, axis=1)[..., None]
    return vals.transpose(0, 1, 3, 2).reshape(g * 512, n)
def pack4(w):
    words, scales = pack_weight(w, "e2m1")
    return words.reshape(words.shape[0], 128, -1), scales


def unpack4(words, scales):
    return unpack_weight(words.reshape(words.shape[0], 128, -1, 2), scales, "e2m1")


T, C, N, R = 2048, 1024, 1024, 1024


def draw0():
    s = mx_kscale(C)
    u = mx_kscale(T)
    echo = np.random.standard_normal((T, C)) * s * u[:, None]
    steer = np.random.standard_normal((C, N)) / np.sqrt(C) / s[:, None]
    stored = np.random.standard_normal((T, R)) / np.sqrt(T) / u[:, None]
    ref_words, ref_scales = pack4(stored)
    return {
        "echo": bf(echo),
        "steer": bf(steer),
        "ref_words": ref_words,
        "ref_scales": ref_scales,
        "col_gain": bf(1 + 0.1 * np.random.standard_normal(N)),
        "row_gain": bf(1 + 0.1 * np.random.standard_normal(R)),
    }


def core(echo, steer, ref_words, ref_scales, col_gain, row_gain):
    y = mxq(f64(echo), 1, "e4m3") @ mxq(f64(steer), 0, "e4m3")
    d = y * f64(col_gain)[None, :]
    stored = unpack4(ref_words, ref_scales)
    c = stored.T @ mxq(d, 0, "e4m3")
    e = c * f64(row_gain)[:, None]
    return np.square(e)


def e4m3fn_bytes(y):
    return np.clip(np.asarray(y, np.float64), -448.0, 448.0).astype(np.float32).astype(ml_dtypes.float8_e4m3fn).view(np.uint8)


def e4m3fn_values(b):
    return np.asarray(b, np.uint8).view(ml_dtypes.float8_e4m3fn).astype(np.float64)


def setup_inputs():
    d = draw0()
    x0 = np.asarray(d['steer']).astype(np.float64)
    s = (np.max(np.abs(x0), axis=(1,), keepdims=True) / 448.0).astype(np.float32)
    out = {}
    for k, v in d.items():
        if k == 'steer':
            out['steer_bytes'] = e4m3fn_bytes(x0 / s.astype(np.float64))
            out['steer_scale'] = s
        else:
            out[k] = v
    return out


def reference(echo, steer_bytes, steer_scale, ref_words, ref_scales, col_gain, row_gain):
    return core(echo, e4m3fn_values(steer_bytes) * steer_scale.astype(np.float64), ref_words, ref_scales, col_gain, row_gain)

@@ -1,0 +1,291 @@
+from contextlib import ExitStack
+
+import concourse.mybir as mybir
+from concourse.masks import make_identity
+
+T, C, N, R = 2048, 1024, 1024, 1024
+FLOPS = 2 * T * C * N + 2 * T * R * N
+
+F32 = mybir.dt.float32
+BF16 = mybir.dt.bfloat16
+U32 = mybir.dt.uint32
+I32 = mybir.dt.int32
+U8 = mybir.dt.uint8
+FP8 = mybir.dt.float8_e4m3fn
+FP8X4 = mybir.dt.float8_e4m3fn_x4
+FP4X4 = mybir.dt.float4_e2m1fn_x4
+COPY = mybir.ActivationFunctionType.Copy
+SQUARE = mybir.ActivationFunctionType.Square
+MULT = mybir.AluOpType.mult
+
+P = 128
+G = T // 512
+CP = C // 512
+HALF = 512
+SORTED = (2, 3)
+
+
+def tile_sonar_ping_coherence_s13_kernel(tc, echo, steer_bytes, steer_scale, ref_words, ref_scales, col_gain, row_gain, out):
+    nc = tc.nc
+    with ExitStack() as ctx:
+        keep = ctx.enter_context(tc.tile_pool(name="keep", bufs=1))
+        ring = ctx.enter_context(tc.tile_pool(name="ring", bufs=4))
+        stage = ctx.enter_context(tc.tile_pool(name="stage", bufs=8))
+        psum = ctx.enter_context(tc.psum_pool(name="psum", bufs=4))
+        ctx.enter_context(tc.manual_schedule())
+
+        eraw = [keep.tile([P, 4, C], BF16, name="eraw%d" % g, align_bytes=64) for g in range(G)]
+        egrp = [keep.tile([P, 2, C], BF16, name="egrp%d" % j, align_bytes=64) for j in range(2 * G)]
+        ecod = [keep.tile([P, 4 * CP * P], U32, name="ecod%d" % g, align_bytes=64) for g in range(G)]
+        escl = [keep.tile([P, 4 * CP * P], U8, name="escl%d" % g, align_bytes=64) for g in range(G)]
+        esort = {g: keep.tile([P, 4, C // 2], F32, name="esort%d" % g, align_bytes=64) for g in SORTED}
+        sraw = keep.tile([P, CP, 4, N], U8, name="sraw", align_bytes=64)
+        sscl = keep.tile([P, CP, 4], F32, name="sscl", align_bytes=64)
+        swide = [keep.tile([P, 4, HALF], BF16, name="swide%d" % j, align_bytes=64) for j in range(2 * CP)]
+        sgrp = [keep.tile([P, HALF, 4], BF16, name="sgrp%d" % j, align_bytes=64) for j in range(2 * CP)]
+        scod = [keep.tile([P, N], U32, name="scod%d" % c, align_bytes=64) for c in range(CP)]
+        sqsc = [keep.tile([P, N], U8, name="sqsc%d" % c, align_bytes=64) for c in range(CP)]
+        dcod = [keep.tile([P, N], U32, name="dcod%d" % g, align_bytes=64) for g in range(G)]
+        dscl = [keep.tile([P, N], U8, name="dscl%d" % g, align_bytes=64) for g in range(G)]
+        pcod = keep.tile([P, G, 2 * R], U8, name="pcod", align_bytes=64)
+        pscl = keep.tile([P, G, R], U8, name="pscl", align_bytes=64)
+        gains = keep.tile([P, N + P], BF16, name="gains", align_bytes=64)
+        ones = keep.tile([P, P], BF16, name="ones", align_bytes=64)
+        idf = keep.tile([P, P], F32, name="idf", align_bytes=64)
+        idb = keep.tile([P, P], BF16, name="idb", align_bytes=64)
+        cgain = keep.tile([P, N], F32, name="cgain", align_bytes=64)
+        rgain = keep.tile([P, R // P], F32, name="rgain", align_bytes=64)
+
+        def bank(tag):
+            return psum.tile([P, 512], F32, name="bank_" + tag, tag=tag)
+
+        nc.gpsimd.memset(gains[:], 0.0)
+        make_identity(nc, idf[:])
+        nc.vector.memset(ones[:], 1.0)
+        nc.vector.memset(pscl[:].rearrange("p g n -> p (g n)").bitcast(I32), 0)
+        nc.gpsimd.tensor_copy(out=idb[:], in_=idf[:])
+
+        echo_g = echo.rearrange("(g p t) k -> g p t k", p=P, t=4)
+        steer_c = steer_bytes.rearrange("(c p t) n -> c p t n", p=P, t=4)
+
+        def load_echo(g, t0, t1):
+            nc.sync.dma_start(out=eraw[g][:, t0:t1, :], in_=echo_g[g][:, t0:t1, :])
+
+        def load_steer(c, h):
+            cols = slice(h * HALF, (h + 1) * HALF)
+            nc.sync.dma_start(out=sraw[:, c, :, cols], in_=steer_c[c][:, :, cols])
+
+        nc.scalar.dma_start(out=sscl[:], in_=steer_scale.rearrange("(c p t) o -> p c (t o)", p=P, t=4))
+        nc.scalar.dma_start(out=gains[0:1, 0:N], in_=col_gain.unsqueeze(0))
+        nc.scalar.dma_start(out=gains[0 : R // P, N : N + P], in_=row_gain.rearrange("(c m) -> c m", m=P))
+        load_steer(0, 0)
+        load_steer(1, 0)
+        for t in range(4):
+            load_echo(0, t, t + 1)
+        for g in range(1, G):
+            load_echo(g, 0, 2)
+            load_echo(g, 2, 4)
+        load_steer(0, 1)
+        load_steer(1, 1)
+        for g in range(G):
+            nc.sync.dma_start(out=pcod[:, g, :].bitcast(I32), in_=ref_words[g].bitcast(I32))
+        for q in range(4):
+            nc.sync.dma_start(
+                out=pscl[32 * q : 32 * q + 4, :, :].bitcast(I32),
+                in_=ref_scales[:, 4 * q : 4 * q + 4, :].rearrange("g r n -> r g n").bitcast(I32),
+            )
+
+        def widen(c, h, ts, on_vector):
+            dst = swide[2 * c + h]
+            for t in ts:
+                src = sraw[:, c, t, h * HALF : (h + 1) * HALF].bitcast(FP8)
+                if on_vector:
+                    nc.vector.tensor_scalar(out=dst[:, t, :], in0=src, scalar1=sscl[:, c, t : t + 1], scalar2=None, op0=MULT)
+                else:
+                    nc.scalar.activation(out=dst[:, t, :], in_=src, func=COPY, scale=sscl[:, c, t : t + 1])
+
+        def interleave(c, h, on_vector):
+            src = swide[2 * c + h][:].rearrange("p t (n i) -> p n t i", i=4)
+            dst = sgrp[2 * c + h][:].rearrange("p (n i) t -> p n t i", i=4)
+            if on_vector:
+                nc.vector.tensor_copy(out=dst, in_=src)
+            else:
+                nc.scalar.copy(out=dst, in_=src)
+
+        def quant_steer(c, h):
+            cols = slice(h * HALF, (h + 1) * HALF)
+            nc.vector.quantize_mx(out=scod[c][:, cols].bitcast(FP8X4), scales=sqsc[c][:, cols], in_=sgrp[2 * c + h][:].rearrange("p n t -> p (n t)"))
+
+        def sort_words(g, t):
+            if g in SORTED:
+                words = eraw[g][:, t, :].bitcast(F32)
+                nc.vector.tensor_copy(out=esort[g][:, t, :].rearrange("p (c u m) -> p c u m", c=CP, u=2), in_=words.rearrange("p (c m u) -> p c u m", c=CP, u=2))
+
+        def turn(g, t):
+            xt = bank("a")
+            words = eraw[g][:, t, :].bitcast(F32)
+            for c in range(CP):
+                for u in range(2):
+                    j = 2 * c + u
+                    src = esort[g][:, t, j * P : (j + 1) * P] if g in SORTED else words[:, 256 * c + u : 256 * (c + 1) : 2]
+                    nc.tensor.transpose(xt[:, j * P : (j + 1) * P], src, idf[:])
+            dst = egrp[2 * g + t // 2][:, t % 2, :].bitcast(F32)
+            nc.scalar.copy(out=dst.rearrange("p (c r u) -> p c r u", c=CP, u=2), in_=xt[:].rearrange("p (c u r) -> p c r u", c=CP, u=2))
+
+        def quant_echo(g, half):
+            cols = slice(half * 512, (half + 1) * 512)
+            nc.vector.quantize_mx(out=ecod[g][:, cols].bitcast(FP8X4), scales=escl[g][:, cols], in_=egrp[2 * g + half][:].rearrange("p t k -> p (t k)"))
+
+        ybank = {}
+        dgrp = {}
+
+        def first(g, b):
+            y = bank("b")
+            ybank[(g, b)] = y
+            ncols = slice(b * P, (b + 1) * P)
+            for t in range(4):
+                for c in range(CP):
+                    ecols = slice((t * CP + c) * P, (t * CP + c + 1) * P)
+                    nc.tensor.matmul_mx(
+                        out=y[:, t * P : (t + 1) * P],
+                        lhsT=ecod[g][:, ecols].bitcast(FP8X4),
+                        lhsT_scale=escl[g][:, ecols],
+                        rhs=scod[c][:, ncols].bitcast(FP8X4),
+                        rhs_scale=sqsc[c][:, ncols],
+                        start=(c == 0),
+                        stop=(c == CP - 1),
+                    )
+
+        def gain(g, b):
+            if b % 2 == 0:
+                dgrp[(g, b // 2)] = ring.tile([P, 2, P, 4], BF16, name="dgrp", tag="dgrp", align_bytes=64)
+            d = dgrp[(g, b // 2)]
+            nc.vector.tensor_tensor(
+                out=d[:, b % 2, :, :],
+                in0=ybank[(g, b)][:].rearrange("p (t n) -> p n t", t=4),
+                in1=cgain[:, b * P : (b + 1) * P].unsqueeze(2).to_broadcast([P, P, 4]),
+                op=MULT,
+            )
+
+        def quant_d(g, b2):
+            cols = slice(b2 * 2 * P, (b2 + 1) * 2 * P)
+            nc.vector.quantize_mx(out=dcod[g][:, cols].bitcast(FP8X4), scales=dscl[g][:, cols], in_=dgrp[(g, b2)][:].rearrange("p b n t -> p (b n t)"))
+
+        acc = {}
+
+        def second(i, h, g):
+            if g == 0:
+                acc[(i, h)] = bank("a")
+            ncols = slice(h * HALF, (h + 1) * HALF)
+            nc.tensor.matmul_mx(
+                out=acc[(i, h)][:],
+                lhsT=pcod[:, g, i * 2 * P : (i + 1) * 2 * P].bitcast(FP4X4),
+                lhsT_scale=pscl[:, g, i * P : (i + 1) * P],
+                rhs=dcod[g][:, ncols].bitcast(FP8X4),
+                rhs_scale=dscl[g][:, ncols],
+                start=(g == 0),
+                stop=(g == G - 1),
+            )
+
+        def finish(i, h):
+            o = stage.tile([P, HALF], F32, name="o", tag="o")
+            nc.scalar.activation(out=o[:], in_=acc[(i, h)][:], func=SQUARE, scale=rgain[:, i : i + 1])
+            nc.sync.dma_start(out=out[i * P : (i + 1) * P, h * HALF : (h + 1) * HALF], in_=o[:])
+
+        for j in range(2):
+            pg = bank("b")
+            nc.tensor.matmul(out=pg[:], lhsT=ones[:], rhs=gains[:, j * 512 : (j + 1) * 512], start=True, stop=True)
+            nc.scalar.copy(out=cgain[:, j * 512 : (j + 1) * 512], in_=pg[:])
+        pr = bank("b")
+        nc.tensor.matmul(out=pr[:, 0 : R // P], lhsT=gains[:, N : N + P], rhs=idb[:, 0 : R // P], start=True, stop=True)
+        nc.scalar.copy(out=rgain[:], in_=pr[:, 0 : R // P])
+
+        widen(0, 0, (0, 1), True)
+        widen(0, 0, (2, 3), False)
+        widen(1, 0, (0, 1), True)
+        widen(1, 0, (2, 3), False)
+        interleave(0, 0, True)
+        for t in range(4):
+            turn(0, t)
+        interleave(1, 0, True)
+        quant_steer(0, 0)
+        quant_echo(0, 0)
+        quant_steer(1, 0)
+        quant_echo(0, 1)
+
+        q = []
+
+        def y(g, b):
+            first(g, b)
+            gain(g, b)
+            while q:
+                quant_d(*q.pop())
+            if b % 2 == 1:
+                q.append((g, b // 2))
+
+        def flush():
+            while q:
+                quant_d(*q.pop())
+
+        for t in range(4):
+            turn(1, t)
+        for t in range(4):
+            sort_words(2, t)
+        quant_echo(1, 0)
+        quant_echo(1, 1)
+        for b in range(2):
+            y(0, b)
+        for t in range(4):
+            sort_words(3, t)
+        for b in range(2, 4):
+            y(0, b)
+        for t in range(4):
+            turn(2, t)
+        for b in range(2):
+            y(1, b)
+        quant_echo(2, 0)
+        quant_echo(2, 1)
+        for t in range(4):
+            turn(3, t)
+        for b in range(2, 4):
+            y(1, b)
+        quant_echo(3, 0)
+        quant_echo(3, 1)
+        for c in range(CP):
+            widen(c, 1, range(4), False)
+        for c in range(CP):
+            interleave(c, 1, False)
+        for i in range(4):
+            second(i, 0, 0)
+        for b in range(4):
+            y(2, b)
+        for i in range(4):
+            second(i, 0, 1)
+        for b in range(4):
+            y(3, b)
+        for i in range(4):
+            second(i, 0, 2)
+        quant_steer(0, 1)
+        flush()
+        quant_steer(1, 1)
+        for i in range(4):
+            second(i, 0, 3)
+            finish(i, 0)
+        for g in range(4):
+            for b in range(4, 8):
+                y(g, b)
+            for g2 in range(4):
+                second(4 + g, 0, g2)
+            finish(4 + g, 0)
+            if g == 3:
+                flush()
+        for i in range(3):
+            for g2 in range(3):
+                second(i, 1, g2)
+        for i in range(3):
+            second(i, 1, 3)
+            finish(i, 1)
+        for i in range(3, 8):
+            for g2 in range(4):
+                second(i, 1, g2)
+            finish(i, 1)

@@ -23,6 +23,7 @@ G = T // 512
 CP = C // 512
 HALF = 512
 SORTED = (2, 3)
+HEAT = 8
 
 
 def tile_sonar_ping_coherence_s13_kernel(tc, echo, steer_bytes, steer_scale, ref_words, ref_scales, col_gain, row_gain, out):
@@ -51,6 +52,7 @@ def tile_sonar_ping_coherence_s13_kernel(tc, echo, steer_bytes, steer_scale, ref
         pscl = keep.tile([P, G, R], U8, name="pscl", align_bytes=64)
         gains = keep.tile([P, N + P], BF16, name="gains", align_bytes=64)
         ones = keep.tile([P, P], BF16, name="ones", align_bytes=64)
+        warm = keep.tile([P, 512], BF16, name="warm", align_bytes=64)
         idf = keep.tile([P, P], F32, name="idf", align_bytes=64)
         idb = keep.tile([P, P], BF16, name="idb", align_bytes=64)
         cgain = keep.tile([P, N], F32, name="cgain", align_bytes=64)
@@ -59,9 +61,10 @@ def tile_sonar_ping_coherence_s13_kernel(tc, echo, steer_bytes, steer_scale, ref
         def bank(tag):
             return psum.tile([P, 512], F32, name="bank_" + tag, tag=tag)
 
+        nc.vector.memset(ones[:], 1.0)
+        nc.vector.memset(warm[:], 0.0)
         nc.gpsimd.memset(gains[:], 0.0)
         make_identity(nc, idf[:])
-        nc.vector.memset(ones[:], 1.0)
         nc.vector.memset(pscl[:].rearrange("p g n -> p (g n)").bitcast(I32), 0)
         nc.gpsimd.tensor_copy(out=idb[:], in_=idf[:])
 
@@ -189,9 +192,19 @@ def tile_sonar_ping_coherence_s13_kernel(tc, echo, steer_bytes, steer_scale, ref
 
         def finish(i, h):
             o = stage.tile([P, HALF], F32, name="o", tag="o")
-            nc.scalar.activation(out=o[:], in_=acc[(i, h)][:], func=SQUARE, scale=rgain[:, i : i + 1])
-            nc.sync.dma_start(out=out[i * P : (i + 1) * P, h * HALF : (h + 1) * HALF], in_=o[:])
+            parts = 2 if (i, h) == (7, 1) else 1
+            w = HALF // parts
+            for j in range(parts):
+                cols = slice(j * w, (j + 1) * w)
+                nc.scalar.activation(out=o[:, cols], in_=acc[(i, h)][:, cols], func=SQUARE, scale=rgain[:, i : i + 1])
+                nc.sync.dma_start(out=out[i * P : (i + 1) * P, h * HALF + j * w : h * HALF + (j + 1) * w], in_=o[:, cols])
 
+        def heat(n, width):
+            w = bank("b")
+            for j in range(n):
+                nc.tensor.matmul(out=w[:, 0:width], lhsT=ones[:], rhs=warm[:, 0:width], start=True, stop=True)
+
+        heat(HEAT, 512)
         for j in range(2):
             pg = bank("b")
             nc.tensor.matmul(out=pg[:], lhsT=ones[:], rhs=gains[:, j * 512 : (j + 1) * 512], start=True, stop=True)
@@ -207,6 +220,7 @@ def tile_sonar_ping_coherence_s13_kernel(tc, echo, steer_bytes, steer_scale, ref
         interleave(0, 0, True)
         for t in range(4):
             turn(0, t)
+            heat(1, 384)
         interleave(1, 0, True)
         quant_steer(0, 0)
         quant_echo(0, 0)
@@ -229,6 +243,7 @@ def tile_sonar_ping_coherence_s13_kernel(tc, echo, steer_bytes, steer_scale, ref
 
         for t in range(4):
             turn(1, t)
+            heat(1, 384)
         for t in range(4):
             sort_words(2, t)
         quant_echo(1, 0)

@@ -23,7 +23,7 @@ G = T // 512
 CP = C // 512
 HALF = 512
 SORTED = (2, 3)
-HEAT = 8
+HEAT = 6
 
 
 def tile_sonar_ping_coherence_s13_kernel(tc, echo, steer_bytes, steer_scale, ref_words, ref_scales, col_gain, row_gain, out):
@@ -61,9 +61,9 @@ def tile_sonar_ping_coherence_s13_kernel(tc, echo, steer_bytes, steer_scale, ref
         def bank(tag):
             return psum.tile([P, 512], F32, name="bank_" + tag, tag=tag)
 
+        nc.vector.memset(gains[:], 0.0)
         nc.vector.memset(ones[:], 1.0)
         nc.vector.memset(warm[:], 0.0)
-        nc.gpsimd.memset(gains[:], 0.0)
         make_identity(nc, idf[:])
         nc.vector.memset(pscl[:].rearrange("p g n -> p (g n)").bitcast(I32), 0)
         nc.gpsimd.tensor_copy(out=idb[:], in_=idf[:])
@@ -78,13 +78,13 @@ def tile_sonar_ping_coherence_s13_kernel(tc, echo, steer_bytes, steer_scale, ref
             cols = slice(h * HALF, (h + 1) * HALF)
             nc.sync.dma_start(out=sraw[:, c, :, cols], in_=steer_c[c][:, :, cols])
 
-        nc.scalar.dma_start(out=sscl[:], in_=steer_scale.rearrange("(c p t) o -> p c (t o)", p=P, t=4))
-        nc.scalar.dma_start(out=gains[0:1, 0:N], in_=col_gain.unsqueeze(0))
-        nc.scalar.dma_start(out=gains[0 : R // P, N : N + P], in_=row_gain.rearrange("(c m) -> c m", m=P))
         load_steer(0, 0)
         load_steer(1, 0)
         for t in range(4):
             load_echo(0, t, t + 1)
+        nc.scalar.dma_start(out=sscl[:], in_=steer_scale.rearrange("(c p t) o -> p c (t o)", p=P, t=4))
+        nc.scalar.dma_start(out=gains[0:1, 0:N], in_=col_gain.unsqueeze(0))
+        nc.scalar.dma_start(out=gains[0 : R // P, N : N + P], in_=row_gain.rearrange("(c m) -> c m", m=P))
         for g in range(1, G):
             load_echo(g, 0, 2)
             load_echo(g, 2, 4)
@@ -122,7 +122,7 @@ def tile_sonar_ping_coherence_s13_kernel(tc, echo, steer_bytes, steer_scale, ref
         def sort_words(g, t):
             if g in SORTED:
                 words = eraw[g][:, t, :].bitcast(F32)
-                nc.vector.tensor_copy(out=esort[g][:, t, :].rearrange("p (c u m) -> p c u m", c=CP, u=2), in_=words.rearrange("p (c m u) -> p c u m", c=CP, u=2))
+                nc.scalar.copy(out=esort[g][:, t, :].rearrange("p (c u m) -> p c u m", c=CP, u=2), in_=words.rearrange("p (c m u) -> p c u m", c=CP, u=2))
 
         def turn(g, t):
             xt = bank("a")
@@ -204,28 +204,19 @@ def tile_sonar_ping_coherence_s13_kernel(tc, echo, steer_bytes, steer_scale, ref
             for j in range(n):
                 nc.tensor.matmul(out=w[:, 0:width], lhsT=ones[:], rhs=warm[:, 0:width], start=True, stop=True)
 
-        heat(HEAT, 512)
-        for j in range(2):
-            pg = bank("b")
-            nc.tensor.matmul(out=pg[:], lhsT=ones[:], rhs=gains[:, j * 512 : (j + 1) * 512], start=True, stop=True)
-            nc.scalar.copy(out=cgain[:, j * 512 : (j + 1) * 512], in_=pg[:])
-        pr = bank("b")
-        nc.tensor.matmul(out=pr[:, 0 : R // P], lhsT=gains[:, N : N + P], rhs=idb[:, 0 : R // P], start=True, stop=True)
-        nc.scalar.copy(out=rgain[:], in_=pr[:, 0 : R // P])
+        gbank = {}
 
-        widen(0, 0, (0, 1), True)
-        widen(0, 0, (2, 3), False)
-        widen(1, 0, (0, 1), True)
-        widen(1, 0, (2, 3), False)
-        interleave(0, 0, True)
-        for t in range(4):
-            turn(0, t)
-            heat(1, 384)
-        interleave(1, 0, True)
-        quant_steer(0, 0)
-        quant_echo(0, 0)
-        quant_steer(1, 0)
-        quant_echo(0, 1)
+        def spread_gain(j):
+            gbank[j] = bank("b")
+            nc.tensor.matmul(out=gbank[j][:], lhsT=ones[:], rhs=gains[:, j * 512 : (j + 1) * 512], start=True, stop=True)
+
+        def keep_gain(j):
+            nc.scalar.copy(out=cgain[:, j * 512 : (j + 1) * 512], in_=gbank[j][:])
+
+        def row_gains():
+            pr = bank("b")
+            nc.tensor.matmul(out=pr[:, 0 : R // P], lhsT=gains[:, N : N + P], rhs=idb[:, 0 : R // P], start=True, stop=True)
+            nc.scalar.copy(out=rgain[:], in_=pr[:, 0 : R // P])
 
         q = []
 
@@ -241,66 +232,96 @@ def tile_sonar_ping_coherence_s13_kernel(tc, echo, steer_bytes, steer_scale, ref
             while q:
                 quant_d(*q.pop())
 
+        def partial(g, n=4):
+            for i in range(n):
+                second(i, 0, g)
+
+        def whole(i, h):
+            for g in range(G):
+                second(i, h, g)
+            finish(i, h)
+
+        heat(HEAT, 512)
+        spread_gain(0)
+        widen(0, 0, (0, 1), True)
+        widen(0, 0, (2, 3), False)
+        widen(1, 0, (0, 1), True)
+        widen(1, 0, (2, 3), False)
+        interleave(0, 0, True)
+        interleave(1, 0, True)
+        for t in range(4):
+            turn(0, t)
+        keep_gain(0)
+        quant_steer(0, 0)
+        quant_echo(0, 0)
+        quant_steer(1, 0)
+        quant_echo(0, 1)
         for t in range(4):
             turn(1, t)
-            heat(1, 384)
         for t in range(4):
             sort_words(2, t)
+        y(0, 0)
+        y(0, 1)
         quant_echo(1, 0)
+        y(0, 2)
         quant_echo(1, 1)
-        for b in range(2):
-            y(0, b)
-        for t in range(4):
-            sort_words(3, t)
-        for b in range(2, 4):
-            y(0, b)
+        y(0, 3)
         for t in range(4):
             turn(2, t)
-        for b in range(2):
-            y(1, b)
+        for t in range(4):
+            sort_words(3, t)
+        y(1, 0)
+        y(1, 1)
         quant_echo(2, 0)
+        y(1, 2)
         quant_echo(2, 1)
+        y(1, 3)
         for t in range(4):
             turn(3, t)
-        for b in range(2, 4):
-            y(1, b)
+        spread_gain(1)
+        row_gains()
+        keep_gain(1)
+        widen(0, 1, range(4), False)
+        widen(1, 1, range(4), False)
+        flush()
         quant_echo(3, 0)
         quant_echo(3, 1)
-        for c in range(CP):
-            widen(c, 1, range(4), False)
-        for c in range(CP):
-            interleave(c, 1, False)
-        for i in range(4):
-            second(i, 0, 0)
-        for b in range(4):
+        for b in range(2):
             y(2, b)
-        for i in range(4):
-            second(i, 0, 1)
-        for b in range(4):
+        partial(0)
+        for b in range(2, 4):
+            y(2, b)
+        for b in range(2):
             y(3, b)
-        for i in range(4):
-            second(i, 0, 2)
-        quant_steer(0, 1)
+        partial(1)
+        for b in range(2, 4):
+            y(3, b)
+        partial(2)
         flush()
+        interleave(0, 1, True)
+        interleave(1, 1, True)
+        quant_steer(0, 1)
         quant_steer(1, 1)
+        partial(3)
         for i in range(4):
-            second(i, 0, 3)
             finish(i, 0)
-        for g in range(4):
+        whole(4, 0)
+        whole(5, 0)
+        for g in range(G):
             for b in range(4, 8):
                 y(g, b)
-            for g2 in range(4):
-                second(4 + g, 0, g2)
-            finish(4 + g, 0)
-            if g == 3:
-                flush()
-        for i in range(3):
-            for g2 in range(3):
-                second(i, 1, g2)
-        for i in range(3):
-            second(i, 1, 3)
+            if g == 0:
+                whole(6, 0)
+            if g == 1:
+                whole(7, 0)
+            if g > 1:
+                for i in range(4):
+                    second(i, 1, g - 2)
+        flush()
+        for g in range(2, G):
+            for i in range(4):
+                second(i, 1, g)
+        for i in range(4):
             finish(i, 1)
-        for i in range(3, 8):
-            for g2 in range(4):
-                second(i, 1, g2)
-            finish(i, 1)
+        for i in range(4, 8):
+            whole(i, 1)

@@ -32,11 +32,12 @@ def tile_sonar_ping_coherence_s13_kernel(tc, echo, steer_bytes, steer_scale, ref
         keep = ctx.enter_context(tc.tile_pool(name="keep", bufs=1))
         ring = ctx.enter_context(tc.tile_pool(name="ring", bufs=4))
         stage = ctx.enter_context(tc.tile_pool(name="stage", bufs=8))
+        lift = ctx.enter_context(tc.tile_pool(name="lift", bufs=2))
         psum = ctx.enter_context(tc.psum_pool(name="psum", bufs=4))
         ctx.enter_context(tc.manual_schedule())
 
         eraw = [keep.tile([P, 4, C], BF16, name="eraw%d" % g, align_bytes=64) for g in range(G)]
-        egrp = [keep.tile([P, 2, C], BF16, name="egrp%d" % j, align_bytes=64) for j in range(2 * G)]
+        egrp = {}
         ecod = [keep.tile([P, 4 * CP * P], U32, name="ecod%d" % g, align_bytes=64) for g in range(G)]
         escl = [keep.tile([P, 4 * CP * P], U8, name="escl%d" % g, align_bytes=64) for g in range(G)]
         esort = {g: keep.tile([P, 4, C // 2], F32, name="esort%d" % g, align_bytes=64) for g in SORTED}
@@ -88,15 +89,20 @@ def tile_sonar_ping_coherence_s13_kernel(tc, echo, steer_bytes, steer_scale, ref
         for g in range(1, G):
             load_echo(g, 0, 2)
             load_echo(g, 2, 4)
+        def load_words(g):
+            nc.sync.dma_start(out=pcod[:, g, :].bitcast(I32), in_=ref_words[g].bitcast(I32))
+
+        load_words(0)
+        for q4 in range(4):
+            nc.sync.dma_start(
+                out=pscl[32 * q4 : 32 * q4 + 4, :, :].bitcast(I32),
+                in_=ref_scales[:, 4 * q4 : 4 * q4 + 4, :].rearrange("g r n -> r g n").bitcast(I32),
+            )
+        load_words(1)
         load_steer(0, 1)
         load_steer(1, 1)
-        for g in range(G):
-            nc.sync.dma_start(out=pcod[:, g, :].bitcast(I32), in_=ref_words[g].bitcast(I32))
-        for q in range(4):
-            nc.sync.dma_start(
-                out=pscl[32 * q : 32 * q + 4, :, :].bitcast(I32),
-                in_=ref_scales[:, 4 * q : 4 * q + 4, :].rearrange("g r n -> r g n").bitcast(I32),
-            )
+        load_words(2)
+        load_words(3)
 
         def widen(c, h, ts, on_vector):
             dst = swide[2 * c + h]
@@ -132,6 +138,8 @@ def tile_sonar_ping_coherence_s13_kernel(tc, echo, steer_bytes, steer_scale, ref
                     j = 2 * c + u
                     src = esort[g][:, t, j * P : (j + 1) * P] if g in SORTED else words[:, 256 * c + u : 256 * (c + 1) : 2]
                     nc.tensor.transpose(xt[:, j * P : (j + 1) * P], src, idf[:])
+            if t % 2 == 0:
+                egrp[2 * g + t // 2] = ring.tile([P, 2, C], BF16, name="egrp", tag="egrp", align_bytes=64)
             dst = egrp[2 * g + t // 2][:, t % 2, :].bitcast(F32)
             nc.scalar.copy(out=dst.rearrange("p (c r u) -> p c r u", c=CP, u=2), in_=xt[:].rearrange("p (c u r) -> p c r u", c=CP, u=2))
 
@@ -174,6 +182,36 @@ def tile_sonar_ping_coherence_s13_kernel(tc, echo, steer_bytes, steer_scale, ref
             cols = slice(b2 * 2 * P, (b2 + 1) * 2 * P)
             nc.vector.quantize_mx(out=dcod[g][:, cols].bitcast(FP8X4), scales=dscl[g][:, cols], in_=dgrp[(g, b2)][:].rearrange("p b n t -> p (b n t)"))
 
+        lifted = {}
+
+        def first_wide(g):
+            lifted[g] = lift.tile([P, 4, HALF], F32, name="lifted", tag="lifted", align_bytes=64)
+            for t in range(4):
+                yb = bank("b")
+                for c in range(CP):
+                    ecols = slice((t * CP + c) * P, (t * CP + c + 1) * P)
+                    nc.tensor.matmul_mx(
+                        out=yb[:],
+                        lhsT=ecod[g][:, ecols].bitcast(FP8X4),
+                        lhsT_scale=escl[g][:, ecols],
+                        rhs=scod[c][:, HALF:N].bitcast(FP8X4),
+                        rhs_scale=sqsc[c][:, HALF:N],
+                        start=(c == 0),
+                        stop=(c == CP - 1),
+                    )
+                nc.scalar.copy(out=lifted[g][:, t, :], in_=yb[:])
+
+        def gain_wide(g, b2):
+            d = ring.tile([P, 2, P, 4], BF16, name="dgrp", tag="dgrp", align_bytes=64)
+            dgrp[(g, b2)] = d
+            n0 = (b2 - 2) * 256
+            nc.vector.tensor_tensor(
+                out=d[:].rearrange("p b (n i) t -> p (b n) t i", i=4),
+                in0=lifted[g][:, :, n0 : n0 + 256].rearrange("p t (n i) -> p n t i", i=4),
+                in1=cgain[:, b2 * 256 : (b2 + 1) * 256].rearrange("p (n i) -> p n i", i=4).unsqueeze(2).to_broadcast([P, 64, 4, 4]),
+                op=MULT,
+            )
+
         acc = {}
 
         def second(i, h, g):
@@ -192,12 +230,27 @@ def tile_sonar_ping_coherence_s13_kernel(tc, echo, steer_bytes, steer_scale, ref
 
         def finish(i, h):
             o = stage.tile([P, HALF], F32, name="o", tag="o")
-            parts = 2 if (i, h) == (7, 1) else 1
-            w = HALF // parts
-            for j in range(parts):
-                cols = slice(j * w, (j + 1) * w)
-                nc.scalar.activation(out=o[:, cols], in_=acc[(i, h)][:, cols], func=SQUARE, scale=rgain[:, i : i + 1])
-                nc.sync.dma_start(out=out[i * P : (i + 1) * P, h * HALF + j * w : h * HALF + (j + 1) * w], in_=o[:, cols])
+            nc.scalar.activation(out=o[:], in_=acc[(i, h)][:], func=SQUARE, scale=rgain[:, i : i + 1])
+            nc.sync.dma_start(out=out[i * P : (i + 1) * P, h * HALF : (h + 1) * HALF], in_=o[:])
+
+        def last_tile():
+            i = R // P - 1
+            for j in range(4):
+                part = bank("b")
+                ncols = slice(HALF + j * P, HALF + (j + 1) * P)
+                for g in range(G):
+                    nc.tensor.matmul_mx(
+                        out=part[:, 0:P],
+                        lhsT=pcod[:, g, i * 2 * P : (i + 1) * 2 * P].bitcast(FP4X4),
+                        lhsT_scale=pscl[:, g, i * P : (i + 1) * P],
+                        rhs=dcod[g][:, ncols].bitcast(FP8X4),
+                        rhs_scale=dscl[g][:, ncols],
+                        start=(g == 0),
+                        stop=(g == G - 1),
+                    )
+                o = stage.tile([P, P], F32, name="olast", tag="olast")
+                nc.scalar.activation(out=o[:], in_=part[:, 0:P], func=SQUARE, scale=rgain[:, i : i + 1])
+                nc.sync.dma_start(out=out[i * P : (i + 1) * P, ncols], in_=o[:])
 
         def heat(n, width):
             w = bank("b")
@@ -298,30 +351,29 @@ def tile_sonar_ping_coherence_s13_kernel(tc, echo, steer_bytes, steer_scale, ref
             y(3, b)
         partial(2)
         flush()
-        interleave(0, 1, True)
+        interleave(0, 1, False)
         interleave(1, 1, True)
         quant_steer(0, 1)
         quant_steer(1, 1)
         partial(3)
         for i in range(4):
             finish(i, 0)
-        whole(4, 0)
-        whole(5, 0)
         for g in range(G):
-            for b in range(4, 8):
-                y(g, b)
-            if g == 0:
-                whole(6, 0)
-            if g == 1:
-                whole(7, 0)
-            if g > 1:
-                for i in range(4):
-                    second(i, 1, g - 2)
-        flush()
-        for g in range(2, G):
+            if g != 1:
+                whole(4 + max(0, g - 1), 0)
+            first_wide(g)
+            if g > 0:
+                quant_d(g - 1, 3)
+            gain_wide(g, 2)
+            gain_wide(g, 3)
+            quant_d(g, 2)
+        quant_d(G - 1, 3)
+        whole(7, 0)
+        for g in range(G):
             for i in range(4):
                 second(i, 1, g)
         for i in range(4):
             finish(i, 1)
-        for i in range(4, 8):
+        for i in range(4, 7):
             whole(i, 1)
+        last_tile()

@@ -23,7 +23,7 @@ G = T // 512
 CP = C // 512
 HALF = 512
 SORTED = (2, 3)
-HEAT = 6
+HEAT = 16
 
 
 def tile_sonar_ping_coherence_s13_kernel(tc, echo, steer_bytes, steer_scale, ref_words, ref_scales, col_gain, row_gain, out):
@@ -36,35 +36,34 @@ def tile_sonar_ping_coherence_s13_kernel(tc, echo, steer_bytes, steer_scale, ref
         psum = ctx.enter_context(tc.psum_pool(name="psum", bufs=4))
         ctx.enter_context(tc.manual_schedule())
 
-        eraw = [keep.tile([P, 4, C], BF16, name="eraw%d" % g, align_bytes=64) for g in range(G)]
+        eraw = [keep.tile([P, 4, C], BF16, name="eraw%d" % g, align_bytes=256) for g in range(G)]
         egrp = {}
-        ecod = [keep.tile([P, 4 * CP * P], U32, name="ecod%d" % g, align_bytes=64) for g in range(G)]
-        escl = [keep.tile([P, 4 * CP * P], U8, name="escl%d" % g, align_bytes=64) for g in range(G)]
-        esort = {g: keep.tile([P, 4, C // 2], F32, name="esort%d" % g, align_bytes=64) for g in SORTED}
-        sraw = keep.tile([P, CP, 4, N], U8, name="sraw", align_bytes=64)
-        sscl = keep.tile([P, CP, 4], F32, name="sscl", align_bytes=64)
-        swide = [keep.tile([P, 4, HALF], BF16, name="swide%d" % j, align_bytes=64) for j in range(2 * CP)]
-        sgrp = [keep.tile([P, HALF, 4], BF16, name="sgrp%d" % j, align_bytes=64) for j in range(2 * CP)]
-        scod = [keep.tile([P, N], U32, name="scod%d" % c, align_bytes=64) for c in range(CP)]
-        sqsc = [keep.tile([P, N], U8, name="sqsc%d" % c, align_bytes=64) for c in range(CP)]
-        dcod = [keep.tile([P, N], U32, name="dcod%d" % g, align_bytes=64) for g in range(G)]
-        dscl = [keep.tile([P, N], U8, name="dscl%d" % g, align_bytes=64) for g in range(G)]
-        pcod = keep.tile([P, G, 2 * R], U8, name="pcod", align_bytes=64)
-        pscl = keep.tile([P, G, R], U8, name="pscl", align_bytes=64)
-        gains = keep.tile([P, N + P], BF16, name="gains", align_bytes=64)
-        ones = keep.tile([P, P], BF16, name="ones", align_bytes=64)
-        warm = keep.tile([P, 512], BF16, name="warm", align_bytes=64)
-        idf = keep.tile([P, P], F32, name="idf", align_bytes=64)
-        idb = keep.tile([P, P], BF16, name="idb", align_bytes=64)
-        cgain = keep.tile([P, N], F32, name="cgain", align_bytes=64)
-        rgain = keep.tile([P, R // P], F32, name="rgain", align_bytes=64)
+        ecod = [keep.tile([P, 4 * CP * P], U32, name="ecod%d" % g, align_bytes=256) for g in range(G)]
+        escl = [keep.tile([P, 4 * CP * P], U8, name="escl%d" % g, align_bytes=256) for g in range(G)]
+        esort = {g: keep.tile([P, 4, C // 2], F32, name="esort%d" % g, align_bytes=256) for g in SORTED}
+        sraw = keep.tile([P, CP, 4, N], U8, name="sraw", align_bytes=256)
+        sscl = keep.tile([P, CP, 4], F32, name="sscl", align_bytes=256)
+        swide = [keep.tile([P, 4, HALF], BF16, name="swide%d" % j, align_bytes=256) for j in range(2 * CP)]
+        sgrp = [keep.tile([P, HALF, 4], BF16, name="sgrp%d" % j, align_bytes=256) for j in range(2 * CP)]
+        scod = [keep.tile([P, N], U32, name="scod%d" % c, align_bytes=256) for c in range(CP)]
+        sqsc = [keep.tile([P, N], U8, name="sqsc%d" % c, align_bytes=256) for c in range(CP)]
+        dcod = [keep.tile([P, N], U32, name="dcod%d" % g, align_bytes=256) for g in range(G)]
+        dscl = [keep.tile([P, N], U8, name="dscl%d" % g, align_bytes=256) for g in range(G)]
+        pcod = keep.tile([P, G, 2 * R], U8, name="pcod", align_bytes=256)
+        pscl = keep.tile([P, G, R], U8, name="pscl", align_bytes=256)
+        gains = keep.tile([P, HALF + P], BF16, name="gains", align_bytes=256)
+        ones = keep.tile([P, P], BF16, name="ones", align_bytes=256)
+        idf = keep.tile([P, P], F32, name="idf", align_bytes=256)
+        idb = keep.tile([P, P], BF16, name="idb", align_bytes=256)
+        cgain1 = keep.tile([P, HALF], BF16, name="cgain1", align_bytes=256)
+        cgain = keep.tile([P, HALF], F32, name="cgain", align_bytes=256)
+        rgain = keep.tile([P, R // P], F32, name="rgain", align_bytes=256)
 
         def bank(tag):
             return psum.tile([P, 512], F32, name="bank_" + tag, tag=tag)
 
-        nc.vector.memset(gains[:], 0.0)
         nc.vector.memset(ones[:], 1.0)
-        nc.vector.memset(warm[:], 0.0)
+        nc.vector.memset(gains[:], 0.0)
         make_identity(nc, idf[:])
         nc.vector.memset(pscl[:].rearrange("p g n -> p (g n)").bitcast(I32), 0)
         nc.gpsimd.tensor_copy(out=idb[:], in_=idf[:])
@@ -79,14 +78,16 @@ def tile_sonar_ping_coherence_s13_kernel(tc, echo, steer_bytes, steer_scale, ref
             cols = slice(h * HALF, (h + 1) * HALF)
             nc.sync.dma_start(out=sraw[:, c, :, cols], in_=steer_c[c][:, :, cols])
 
+        nc.scalar.dma_start(out=sscl[:], in_=steer_scale.rearrange("(c p t) o -> p c (t o)", p=P, t=4))
         load_steer(0, 0)
         load_steer(1, 0)
         for t in range(4):
             load_echo(0, t, t + 1)
-        nc.scalar.dma_start(out=sscl[:], in_=steer_scale.rearrange("(c p t) o -> p c (t o)", p=P, t=4))
-        nc.scalar.dma_start(out=gains[0:1, 0:N], in_=col_gain.unsqueeze(0))
-        nc.scalar.dma_start(out=gains[0 : R // P, N : N + P], in_=row_gain.rearrange("(c m) -> c m", m=P))
-        for g in range(1, G):
+        nc.scalar.dma_start(out=gains[0:1, 0:HALF], in_=col_gain[0:HALF].unsqueeze(0))
+        nc.scalar.dma_start(out=gains[0 : R // P, HALF : HALF + P], in_=row_gain.rearrange("(c m) -> c m", m=P))
+        for t in range(4):
+            load_echo(1, t, t + 1)
+        for g in range(2, G):
             load_echo(g, 0, 2)
             load_echo(g, 2, 4)
         def load_words(g):
@@ -101,6 +102,7 @@ def tile_sonar_ping_coherence_s13_kernel(tc, echo, steer_bytes, steer_scale, ref
         load_words(1)
         load_steer(0, 1)
         load_steer(1, 1)
+        nc.sync.dma_start(out=cgain1[:], in_=col_gain[HALF:N].partition_broadcast(P))
         load_words(2)
         load_words(3)
 
@@ -125,10 +127,11 @@ def tile_sonar_ping_coherence_s13_kernel(tc, echo, steer_bytes, steer_scale, ref
             cols = slice(h * HALF, (h + 1) * HALF)
             nc.vector.quantize_mx(out=scod[c][:, cols].bitcast(FP8X4), scales=sqsc[c][:, cols], in_=sgrp[2 * c + h][:].rearrange("p n t -> p (n t)"))
 
-        def sort_words(g, t):
+        def sort_words(g, t, on_vector=False):
             if g in SORTED:
                 words = eraw[g][:, t, :].bitcast(F32)
-                nc.scalar.copy(out=esort[g][:, t, :].rearrange("p (c u m) -> p c u m", c=CP, u=2), in_=words.rearrange("p (c m u) -> p c u m", c=CP, u=2))
+                copy = nc.vector.tensor_copy if on_vector else nc.scalar.copy
+                copy(out=esort[g][:, t, :].rearrange("p (c u m) -> p c u m", c=CP, u=2), in_=words.rearrange("p (c m u) -> p c u m", c=CP, u=2))
 
         def turn(g, t):
             xt = bank("a")
@@ -139,7 +142,7 @@ def tile_sonar_ping_coherence_s13_kernel(tc, echo, steer_bytes, steer_scale, ref
                     src = esort[g][:, t, j * P : (j + 1) * P] if g in SORTED else words[:, 256 * c + u : 256 * (c + 1) : 2]
                     nc.tensor.transpose(xt[:, j * P : (j + 1) * P], src, idf[:])
             if t % 2 == 0:
-                egrp[2 * g + t // 2] = ring.tile([P, 2, C], BF16, name="egrp", tag="egrp", align_bytes=64)
+                egrp[2 * g + t // 2] = ring.tile([P, 2, C], BF16, name="egrp", tag="egrp", align_bytes=256)
             dst = egrp[2 * g + t // 2][:, t % 2, :].bitcast(F32)
             nc.scalar.copy(out=dst.rearrange("p (c r u) -> p c r u", c=CP, u=2), in_=xt[:].rearrange("p (c u r) -> p c r u", c=CP, u=2))
 
@@ -169,7 +172,7 @@ def tile_sonar_ping_coherence_s13_kernel(tc, echo, steer_bytes, steer_scale, ref
 
         def gain(g, b):
             if b % 2 == 0:
-                dgrp[(g, b // 2)] = ring.tile([P, 2, P, 4], BF16, name="dgrp", tag="dgrp", align_bytes=64)
+                dgrp[(g, b // 2)] = ring.tile([P, 2, P, 4], BF16, name="dgrp", tag="dgrp", align_bytes=256)
             d = dgrp[(g, b // 2)]
             nc.vector.tensor_tensor(
                 out=d[:, b % 2, :, :],
@@ -185,7 +188,7 @@ def tile_sonar_ping_coherence_s13_kernel(tc, echo, steer_bytes, steer_scale, ref
         lifted = {}
 
         def first_wide(g):
-            lifted[g] = lift.tile([P, 4, HALF], F32, name="lifted", tag="lifted", align_bytes=64)
+            lifted[g] = lift.tile([P, 4, HALF], F32, name="lifted", tag="lifted", align_bytes=256)
             for t in range(4):
                 yb = bank("b")
                 for c in range(CP):
@@ -202,13 +205,13 @@ def tile_sonar_ping_coherence_s13_kernel(tc, echo, steer_bytes, steer_scale, ref
                 nc.scalar.copy(out=lifted[g][:, t, :], in_=yb[:])
 
         def gain_wide(g, b2):
-            d = ring.tile([P, 2, P, 4], BF16, name="dgrp", tag="dgrp", align_bytes=64)
+            d = ring.tile([P, 2, P, 4], BF16, name="dgrp", tag="dgrp", align_bytes=256)
             dgrp[(g, b2)] = d
             n0 = (b2 - 2) * 256
             nc.vector.tensor_tensor(
                 out=d[:].rearrange("p b (n i) t -> p (b n) t i", i=4),
                 in0=lifted[g][:, :, n0 : n0 + 256].rearrange("p t (n i) -> p n t i", i=4),
-                in1=cgain[:, b2 * 256 : (b2 + 1) * 256].rearrange("p (n i) -> p n i", i=4).unsqueeze(2).to_broadcast([P, 64, 4, 4]),
+                in1=cgain1[:, n0 : n0 + 256].rearrange("p (n i) -> p n i", i=4).unsqueeze(2).to_broadcast([P, 64, 4, 4]),
                 op=MULT,
             )
 
@@ -255,20 +258,16 @@ def tile_sonar_ping_coherence_s13_kernel(tc, echo, steer_bytes, steer_scale, ref
         def heat(n, width):
             w = bank("b")
             for j in range(n):
-                nc.tensor.matmul(out=w[:, 0:width], lhsT=ones[:], rhs=warm[:, 0:width], start=True, stop=True)
-
-        gbank = {}
+                nc.tensor.matmul(out=w[:, 0:width], lhsT=ones[:], rhs=ones[:, 0:width], start=True, stop=True)
 
         def spread_gain(j):
-            gbank[j] = bank("b")
-            nc.tensor.matmul(out=gbank[j][:], lhsT=ones[:], rhs=gains[:, j * 512 : (j + 1) * 512], start=True, stop=True)
-
-        def keep_gain(j):
-            nc.scalar.copy(out=cgain[:, j * 512 : (j + 1) * 512], in_=gbank[j][:])
+            pg = bank("b")
+            nc.tensor.matmul(out=pg[:], lhsT=ones[:], rhs=gains[:, 0:HALF], start=True, stop=True)
+            return pg
 
         def row_gains():
             pr = bank("b")
-            nc.tensor.matmul(out=pr[:, 0 : R // P], lhsT=gains[:, N : N + P], rhs=idb[:, 0 : R // P], start=True, stop=True)
+            nc.tensor.matmul(out=pr[:, 0 : R // P], lhsT=gains[:, HALF : HALF + P], rhs=idb[:, 0 : R // P], start=True, stop=True)
             nc.scalar.copy(out=rgain[:], in_=pr[:, 0 : R // P])
 
         q = []
@@ -294,8 +293,7 @@ def tile_sonar_ping_coherence_s13_kernel(tc, echo, steer_bytes, steer_scale, ref
                 second(i, h, g)
             finish(i, h)
 
-        heat(HEAT, 512)
-        spread_gain(0)
+        heat(HEAT, P)
         widen(0, 0, (0, 1), True)
         widen(0, 0, (2, 3), False)
         widen(1, 0, (0, 1), True)
@@ -304,25 +302,30 @@ def tile_sonar_ping_coherence_s13_kernel(tc, echo, steer_bytes, steer_scale, ref
         interleave(1, 0, True)
         for t in range(4):
             turn(0, t)
-        keep_gain(0)
+        pg = spread_gain(0)
         quant_steer(0, 0)
         quant_echo(0, 0)
         quant_steer(1, 0)
         quant_echo(0, 1)
-        for t in range(4):
-            turn(1, t)
+        turn(1, 0)
+        turn(1, 1)
+        nc.scalar.copy(out=cgain[:], in_=pg[:])
+        turn(1, 2)
+        turn(1, 3)
         for t in range(4):
             sort_words(2, t)
+        quant_echo(1, 0)
         y(0, 0)
         y(0, 1)
-        quant_echo(1, 0)
-        y(0, 2)
         quant_echo(1, 1)
+        y(0, 2)
         y(0, 3)
         for t in range(4):
             turn(2, t)
-        for t in range(4):
-            sort_words(3, t)
+        sort_words(3, 0, True)
+        sort_words(3, 1, True)
+        sort_words(3, 2)
+        sort_words(3, 3)
         y(1, 0)
         y(1, 1)
         quant_echo(2, 0)
@@ -331,9 +334,7 @@ def tile_sonar_ping_coherence_s13_kernel(tc, echo, steer_bytes, steer_scale, ref
         y(1, 3)
         for t in range(4):
             turn(3, t)
-        spread_gain(1)
         row_gains()
-        keep_gain(1)
         widen(0, 1, range(4), False)
         widen(1, 1, range(4), False)
         flush()

from contextlib import ExitStack

import concourse.mybir as mybir
from concourse.masks import make_identity

T, C, N, R = 2048, 1024, 1024, 1024
FLOPS = 2 * T * C * N + 2 * T * R * N

F32 = mybir.dt.float32
BF16 = mybir.dt.bfloat16
U32 = mybir.dt.uint32
I32 = mybir.dt.int32
U8 = mybir.dt.uint8
FP8 = mybir.dt.float8_e4m3fn
FP8X4 = mybir.dt.float8_e4m3fn_x4
FP4X4 = mybir.dt.float4_e2m1fn_x4
COPY = mybir.ActivationFunctionType.Copy
SQUARE = mybir.ActivationFunctionType.Square
MULT = mybir.AluOpType.mult

P = 128
G = T // 512
CP = C // 512
HALF = 512
SORTED = (2, 3)
HEAT = 16


def tile_sonar_ping_coherence_s13_kernel(tc, echo, steer_bytes, steer_scale, ref_words, ref_scales, col_gain, row_gain, out):
    nc = tc.nc
    with ExitStack() as ctx:
        keep = ctx.enter_context(tc.tile_pool(name="keep", bufs=1))
        ring = ctx.enter_context(tc.tile_pool(name="ring", bufs=4))
        stage = ctx.enter_context(tc.tile_pool(name="stage", bufs=8))
        lift = ctx.enter_context(tc.tile_pool(name="lift", bufs=2))
        psum = ctx.enter_context(tc.psum_pool(name="psum", bufs=4))
        ctx.enter_context(tc.manual_schedule())

        eraw = [keep.tile([P, 4, C], BF16, name="eraw%d" % g, align_bytes=256) for g in range(G)]
        egrp = {}
        ecod = [keep.tile([P, 4 * CP * P], U32, name="ecod%d" % g, align_bytes=256) for g in range(G)]
        escl = [keep.tile([P, 4 * CP * P], U8, name="escl%d" % g, align_bytes=256) for g in range(G)]
        esort = {g: keep.tile([P, 4, C // 2], F32, name="esort%d" % g, align_bytes=256) for g in SORTED}
        sraw = keep.tile([P, CP, 4, N], U8, name="sraw", align_bytes=256)
        sscl = keep.tile([P, CP, 4], F32, name="sscl", align_bytes=256)
        swide = [keep.tile([P, 4, HALF], BF16, name="swide%d" % j, align_bytes=256) for j in range(2 * CP)]
        sgrp = [keep.tile([P, HALF, 4], BF16, name="sgrp%d" % j, align_bytes=256) for j in range(2 * CP)]
        scod = [keep.tile([P, N], U32, name="scod%d" % c, align_bytes=256) for c in range(CP)]
        sqsc = [keep.tile([P, N], U8, name="sqsc%d" % c, align_bytes=256) for c in range(CP)]
        dcod = [keep.tile([P, N], U32, name="dcod%d" % g, align_bytes=256) for g in range(G)]
        dscl = [keep.tile([P, N], U8, name="dscl%d" % g, align_bytes=256) for g in range(G)]
        pcod = keep.tile([P, G, 2 * R], U8, name="pcod", align_bytes=256)
        pscl = keep.tile([P, G, R], U8, name="pscl", align_bytes=256)
        gains = keep.tile([P, HALF + P], BF16, name="gains", align_bytes=256)
        ones = keep.tile([P, P], BF16, name="ones", align_bytes=256)
        idf = keep.tile([P, P], F32, name="idf", align_bytes=256)
        idb = keep.tile([P, P], BF16, name="idb", align_bytes=256)
        cgain1 = keep.tile([P, HALF], BF16, name="cgain1", align_bytes=256)
        cgain = keep.tile([P, HALF], F32, name="cgain", align_bytes=256)
        rgain = keep.tile([P, R // P], F32, name="rgain", align_bytes=256)

        def bank(tag):
            return psum.tile([P, 512], F32, name="bank_" + tag, tag=tag)

        nc.vector.memset(ones[:], 1.0)
        nc.vector.memset(gains[:], 0.0)
        make_identity(nc, idf[:])
        nc.vector.memset(pscl[:].rearrange("p g n -> p (g n)").bitcast(I32), 0)
        nc.gpsimd.tensor_copy(out=idb[:], in_=idf[:])

        echo_g = echo.rearrange("(g p t) k -> g p t k", p=P, t=4)
        steer_c = steer_bytes.rearrange("(c p t) n -> c p t n", p=P, t=4)

        def load_echo(g, t0, t1):
            nc.sync.dma_start(out=eraw[g][:, t0:t1, :], in_=echo_g[g][:, t0:t1, :])

        def load_steer(c, h):
            cols = slice(h * HALF, (h + 1) * HALF)
            nc.sync.dma_start(out=sraw[:, c, :, cols], in_=steer_c[c][:, :, cols])

        nc.scalar.dma_start(out=sscl[:], in_=steer_scale.rearrange("(c p t) o -> p c (t o)", p=P, t=4))
        load_steer(0, 0)
        load_steer(1, 0)
        for t in range(4):
            load_echo(0, t, t + 1)
        nc.scalar.dma_start(out=gains[0:1, 0:HALF], in_=col_gain[0:HALF].unsqueeze(0))
        nc.scalar.dma_start(out=gains[0 : R // P, HALF : HALF + P], in_=row_gain.rearrange("(c m) -> c m", m=P))
        for t in range(4):
            load_echo(1, t, t + 1)
        for g in range(2, G):
            load_echo(g, 0, 2)
            load_echo(g, 2, 4)
        def load_words(g):
            nc.sync.dma_start(out=pcod[:, g, :].bitcast(I32), in_=ref_words[g].bitcast(I32))

        load_words(0)
        for q4 in range(4):
            nc.sync.dma_start(
                out=pscl[32 * q4 : 32 * q4 + 4, :, :].bitcast(I32),
                in_=ref_scales[:, 4 * q4 : 4 * q4 + 4, :].rearrange("g r n -> r g n").bitcast(I32),
            )
        load_words(1)
        load_steer(0, 1)
        load_steer(1, 1)
        nc.sync.dma_start(out=cgain1[:], in_=col_gain[HALF:N].partition_broadcast(P))
        load_words(2)
        load_words(3)

        def widen(c, h, ts, on_vector):
            dst = swide[2 * c + h]
            for t in ts:
                src = sraw[:, c, t, h * HALF : (h + 1) * HALF].bitcast(FP8)
                if on_vector:
                    nc.vector.tensor_scalar(out=dst[:, t, :], in0=src, scalar1=sscl[:, c, t : t + 1], scalar2=None, op0=MULT)
                else:
                    nc.scalar.activation(out=dst[:, t, :], in_=src, func=COPY, scale=sscl[:, c, t : t + 1])

        def interleave(c, h, on_vector):
            src = swide[2 * c + h][:].rearrange("p t (n i) -> p n t i", i=4)
            dst = sgrp[2 * c + h][:].rearrange("p (n i) t -> p n t i", i=4)
            if on_vector:
                nc.vector.tensor_copy(out=dst, in_=src)
            else:
                nc.scalar.copy(out=dst, in_=src)

        def quant_steer(c, h):
            cols = slice(h * HALF, (h + 1) * HALF)
            nc.vector.quantize_mx(out=scod[c][:, cols].bitcast(FP8X4), scales=sqsc[c][:, cols], in_=sgrp[2 * c + h][:].rearrange("p n t -> p (n t)"))

        def sort_words(g, t, on_vector=False):
            if g in SORTED:
                words = eraw[g][:, t, :].bitcast(F32)
                copy = nc.vector.tensor_copy if on_vector else nc.scalar.copy
                copy(out=esort[g][:, t, :].rearrange("p (c u m) -> p c u m", c=CP, u=2), in_=words.rearrange("p (c m u) -> p c u m", c=CP, u=2))

        def turn(g, t):
            xt = bank("a")
            words = eraw[g][:, t, :].bitcast(F32)
            for c in range(CP):
                for u in range(2):
                    j = 2 * c + u
                    src = esort[g][:, t, j * P : (j + 1) * P] if g in SORTED else words[:, 256 * c + u : 256 * (c + 1) : 2]
                    nc.tensor.transpose(xt[:, j * P : (j + 1) * P], src, idf[:])
            if t % 2 == 0:
                egrp[2 * g + t // 2] = ring.tile([P, 2, C], BF16, name="egrp", tag="egrp", align_bytes=256)
            dst = egrp[2 * g + t // 2][:, t % 2, :].bitcast(F32)
            nc.scalar.copy(out=dst.rearrange("p (c r u) -> p c r u", c=CP, u=2), in_=xt[:].rearrange("p (c u r) -> p c r u", c=CP, u=2))

        def quant_echo(g, half):
            cols = slice(half * 512, (half + 1) * 512)
            nc.vector.quantize_mx(out=ecod[g][:, cols].bitcast(FP8X4), scales=escl[g][:, cols], in_=egrp[2 * g + half][:].rearrange("p t k -> p (t k)"))

        ybank = {}
        dgrp = {}

        def first(g, b):
            y = bank("b")
            ybank[(g, b)] = y
            ncols = slice(b * P, (b + 1) * P)
            for t in range(4):
                for c in range(CP):
                    ecols = slice((t * CP + c) * P, (t * CP + c + 1) * P)
                    nc.tensor.matmul_mx(
                        out=y[:, t * P : (t + 1) * P],
                        lhsT=ecod[g][:, ecols].bitcast(FP8X4),
                        lhsT_scale=escl[g][:, ecols],
                        rhs=scod[c][:, ncols].bitcast(FP8X4),
                        rhs_scale=sqsc[c][:, ncols],
                        start=(c == 0),
                        stop=(c == CP - 1),
                    )

        def gain(g, b):
            if b % 2 == 0:
                dgrp[(g, b // 2)] = ring.tile([P, 2, P, 4], BF16, name="dgrp", tag="dgrp", align_bytes=256)
            d = dgrp[(g, b // 2)]
            nc.vector.tensor_tensor(
                out=d[:, b % 2, :, :],
                in0=ybank[(g, b)][:].rearrange("p (t n) -> p n t", t=4),
                in1=cgain[:, b * P : (b + 1) * P].unsqueeze(2).to_broadcast([P, P, 4]),
                op=MULT,
            )

        def quant_d(g, b2):
            cols = slice(b2 * 2 * P, (b2 + 1) * 2 * P)
            nc.vector.quantize_mx(out=dcod[g][:, cols].bitcast(FP8X4), scales=dscl[g][:, cols], in_=dgrp[(g, b2)][:].rearrange("p b n t -> p (b n t)"))

        lifted = {}

        def first_wide(g):
            lifted[g] = lift.tile([P, 4, HALF], F32, name="lifted", tag="lifted", align_bytes=256)
            for t in range(4):
                yb = bank("b")
                for c in range(CP):
                    ecols = slice((t * CP + c) * P, (t * CP + c + 1) * P)
                    nc.tensor.matmul_mx(
                        out=yb[:],
                        lhsT=ecod[g][:, ecols].bitcast(FP8X4),
                        lhsT_scale=escl[g][:, ecols],
                        rhs=scod[c][:, HALF:N].bitcast(FP8X4),
                        rhs_scale=sqsc[c][:, HALF:N],
                        start=(c == 0),
                        stop=(c == CP - 1),
                    )
                nc.scalar.copy(out=lifted[g][:, t, :], in_=yb[:])

        def gain_wide(g, b2):
            d = ring.tile([P, 2, P, 4], BF16, name="dgrp", tag="dgrp", align_bytes=256)
            dgrp[(g, b2)] = d
            n0 = (b2 - 2) * 256
            nc.vector.tensor_tensor(
                out=d[:].rearrange("p b (n i) t -> p (b n) t i", i=4),
                in0=lifted[g][:, :, n0 : n0 + 256].rearrange("p t (n i) -> p n t i", i=4),
                in1=cgain1[:, n0 : n0 + 256].rearrange("p (n i) -> p n i", i=4).unsqueeze(2).to_broadcast([P, 64, 4, 4]),
                op=MULT,
            )

        acc = {}

        def second(i, h, g):
            if g == 0:
                acc[(i, h)] = bank("a")
            ncols = slice(h * HALF, (h + 1) * HALF)
            nc.tensor.matmul_mx(
                out=acc[(i, h)][:],
                lhsT=pcod[:, g, i * 2 * P : (i + 1) * 2 * P].bitcast(FP4X4),
                lhsT_scale=pscl[:, g, i * P : (i + 1) * P],
                rhs=dcod[g][:, ncols].bitcast(FP8X4),
                rhs_scale=dscl[g][:, ncols],
                start=(g == 0),
                stop=(g == G - 1),
            )

        def finish(i, h):
            o = stage.tile([P, HALF], F32, name="o", tag="o")
            nc.scalar.activation(out=o[:], in_=acc[(i, h)][:], func=SQUARE, scale=rgain[:, i : i + 1])
            nc.sync.dma_start(out=out[i * P : (i + 1) * P, h * HALF : (h + 1) * HALF], in_=o[:])

        def last_tile():
            i = R // P - 1
            for j in range(4):
                part = bank("b")
                ncols = slice(HALF + j * P, HALF + (j + 1) * P)
                for g in range(G):
                    nc.tensor.matmul_mx(
                        out=part[:, 0:P],
                        lhsT=pcod[:, g, i * 2 * P : (i + 1) * 2 * P].bitcast(FP4X4),
                        lhsT_scale=pscl[:, g, i * P : (i + 1) * P],
                        rhs=dcod[g][:, ncols].bitcast(FP8X4),
                        rhs_scale=dscl[g][:, ncols],
                        start=(g == 0),
                        stop=(g == G - 1),
                    )
                o = stage.tile([P, P], F32, name="olast", tag="olast")
                nc.scalar.activation(out=o[:], in_=part[:, 0:P], func=SQUARE, scale=rgain[:, i : i + 1])
                nc.sync.dma_start(out=out[i * P : (i + 1) * P, ncols], in_=o[:])

        def heat(n, width):
            w = bank("b")
            for j in range(n):
                nc.tensor.matmul(out=w[:, 0:width], lhsT=ones[:], rhs=ones[:, 0:width], start=True, stop=True)

        def spread_gain(j):
            pg = bank("b")
            nc.tensor.matmul(out=pg[:], lhsT=ones[:], rhs=gains[:, 0:HALF], start=True, stop=True)
            return pg

        def row_gains():
            pr = bank("b")
            nc.tensor.matmul(out=pr[:, 0 : R // P], lhsT=gains[:, HALF : HALF + P], rhs=idb[:, 0 : R // P], start=True, stop=True)
            nc.scalar.copy(out=rgain[:], in_=pr[:, 0 : R // P])

        q = []

        def y(g, b):
            first(g, b)
            gain(g, b)
            while q:
                quant_d(*q.pop())
            if b % 2 == 1:
                q.append((g, b // 2))

        def flush():
            while q:
                quant_d(*q.pop())

        def partial(g, n=4):
            for i in range(n):
                second(i, 0, g)

        def whole(i, h):
            for g in range(G):
                second(i, h, g)
            finish(i, h)

        heat(HEAT, P)
        widen(0, 0, (0, 1), True)
        widen(0, 0, (2, 3), False)
        widen(1, 0, (0, 1), True)
        widen(1, 0, (2, 3), False)
        interleave(0, 0, True)
        interleave(1, 0, True)
        for t in range(4):
            turn(0, t)
        pg = spread_gain(0)
        quant_steer(0, 0)
        quant_echo(0, 0)
        quant_steer(1, 0)
        quant_echo(0, 1)
        turn(1, 0)
        turn(1, 1)
        nc.scalar.copy(out=cgain[:], in_=pg[:])
        turn(1, 2)
        turn(1, 3)
        for t in range(4):
            sort_words(2, t)
        quant_echo(1, 0)
        y(0, 0)
        y(0, 1)
        quant_echo(1, 1)
        y(0, 2)
        y(0, 3)
        for t in range(4):
            turn(2, t)
        sort_words(3, 0, True)
        sort_words(3, 1, True)
        sort_words(3, 2)
        sort_words(3, 3)
        y(1, 0)
        y(1, 1)
        quant_echo(2, 0)
        y(1, 2)
        quant_echo(2, 1)
        y(1, 3)
        for t in range(4):
            turn(3, t)
        row_gains()
        widen(0, 1, range(4), False)
        widen(1, 1, range(4), False)
        flush()
        quant_echo(3, 0)
        quant_echo(3, 1)
        for b in range(2):
            y(2, b)
        partial(0)
        for b in range(2, 4):
            y(2, b)
        for b in range(2):
            y(3, b)
        partial(1)
        for b in range(2, 4):
            y(3, b)
        partial(2)
        flush()
        interleave(0, 1, False)
        interleave(1, 1, True)
        quant_steer(0, 1)
        quant_steer(1, 1)
        partial(3)
        for i in range(4):
            finish(i, 0)
        for g in range(G):
            if g != 1:
                whole(4 + max(0, g - 1), 0)
            first_wide(g)
            if g > 0:
                quant_d(g - 1, 3)
            gain_wide(g, 2)
            gain_wide(g, 3)
            quant_d(g, 2)
        quant_d(G - 1, 3)
        whole(7, 0)
        for g in range(G):
            for i in range(4):
                second(i, 1, g)
        for i in range(4):
            finish(i, 1)
        for i in range(4, 7):
            whole(i, 1)
        last_tile()
